import numpy as np
import ml_dtypes

BF16 = ml_dtypes.bfloat16


def bf(x):
    return np.asarray(x, np.float32).astype(BF16)


def f32(x):
    return np.asarray(x, np.float32)


def f64(x):
    return np.asarray(x).astype(np.float64)


def striped(idx):
    return np.tile(idx.reshape(-1, 16).T, (8, 1))


S, K, H, M, N, E, Q = 512, 128, 256, 256, 128, 2, 64


def setup_inputs():
    return {"base": bf(np.random.standard_normal((M, S))), "x": bf(np.random.standard_normal((K, N))), "w": bf(np.random.standard_normal((E, K, H)) / np.sqrt(K)), "b": f32(0.5 * np.random.standard_normal((H, E))), "w2": bf(1.5 * np.random.standard_normal((E, H, M)) / np.sqrt(H)), "c": f32(0.2 + 0.8 * np.random.random_sample((1, N))), "offs": striped(np.random.permutation(S)[:N])}


def reference(base, x, w, b, w2, c, offs):
    idx = offs[:16].T.reshape(-1)
    z = f64(base).copy()
    for e in range(E):
        t = f64(w)[e].T @ f64(x)[:, e * Q : (e + 1) * Q] + f64(b)[:, e : e + 1]
        t = np.maximum(t, 0.0) * f64(c)[:, e * Q : (e + 1) * Q]
        z[:, idx[e * Q : (e + 1) * Q]] += f64(w2)[e].T @ t
    return z

@@ -1,0 +1,76 @@
+import concourse.mybir as mybir
+from concourse.masks import make_identity
+
+BF16, F32, U16 = mybir.dt.bfloat16, mybir.dt.float32, mybir.dt.uint16
+RELU = mybir.ActivationFunctionType.Relu
+MULT = mybir.AluOpType.mult
+
+P = 128
+S = 512
+N = 128
+E = 2
+Q = N // E
+HB = 2
+MB = 2
+COLS = Q // 16
+
+FLOPS = 2 * N * P * (HB * P) + 2 * N * (HB * P) * (MB * P)
+
+
+def tile_rows_ffnback_relu_kernel(tc, base, x, w, b, w2, c, offs, out):
+    nc = tc.nc
+    with (
+        tc.tile_pool(name="held", bufs=1) as held,
+        tc.psum_pool(name="psum", bufs=1) as psum,
+    ):
+        base_t = held.tile([P, MB, S], BF16)
+        nc.sync.dma_start(base_t[:], base.rearrange("(a p) s -> p a s", p=P))
+        x_t = held.tile([P, N], BF16)
+        nc.scalar.dma_start(x_t[:], x)
+        w_t = held.tile([P, E, HB * P], BF16)
+        nc.scalar.dma_start(w_t[:], w.rearrange("e k h -> k e h"))
+        w2_t = held.tile([P, E * HB, MB * P], BF16)
+        nc.sync.dma_start(w2_t[:], w2.rearrange("e (a p) m -> p (e a) m", p=P))
+        offsets = held.tile([P, N // 16], U16)
+        nc.sync.dma_start(offsets[:], offs)
+        b_t = held.tile([P, HB, E], F32)
+        nc.scalar.dma_start(b_t[:], b.rearrange("(a p) e -> p a e", p=P))
+        c_t = held.tile([P, N], F32)
+        nc.scalar.dma_start(c_t[:], c.rearrange("o t -> (o t)").partition_broadcast(P))
+
+        ident = held.tile([P, P], BF16)
+        make_identity(nc, ident[:])
+
+        windows = [psum.tile([P, S], F32, name=f"window{m}") for m in range(MB)]
+        for m in range(MB):
+            nc.tensor.matmul(windows[m][:], ident[:], base_t[:, m, :], start=True, stop=False)
+
+        h = held.tile([P, E, HB, Q], BF16)
+        for e in range(E):
+            entries = slice(e * Q, (e + 1) * Q)
+            pre = psum.tile([P, HB, Q], F32, name=f"pre{e}")
+            act = held.tile([P, HB, Q], F32, name=f"act{e}")
+            for a in range(HB):
+                nc.tensor.matmul(pre[:, a, :], w_t[:, e, a * P : (a + 1) * P], x_t[:, entries], start=True, stop=True)
+            for a in range(HB):
+                nc.scalar.activation(act[:, a, :], pre[:, a, :], RELU, bias=b_t[:, a, e : e + 1])
+            for a in range(HB):
+                nc.vector.tensor_tensor(h[:, e, a, :], act[:, a, :], c_t[:, entries], MULT)
+
+        for m in range(MB):
+            for e in range(E):
+                for a in range(HB):
+                    nc.tensor.matmul(
+                        windows[m][:].indirect(offsets[:, e * COLS : (e + 1) * COLS]),
+                        w2_t[:, e * HB + a, m * P : (m + 1) * P],
+                        h[:, e, a, :],
+                        start=False,
+                        stop=(e == E - 1 and a == HB - 1),
+                    )
+
+        z0 = held.tile([P, S], F32)
+        nc.vector.tensor_copy(z0[:], windows[0][:])
+        nc.sync.dma_start(out[0:P, :], z0[:])
+        z1 = held.tile([P, S], F32)
+        nc.scalar.copy(z1[:], windows[1][:])
+        nc.scalar.dma_start(out[P : 2 * P, :], z1[:])

@@ -2,8 +2,7 @@ import concourse.mybir as mybir
 from concourse.masks import make_identity
 
 BF16, F32, U16 = mybir.dt.bfloat16, mybir.dt.float32, mybir.dt.uint16
-RELU = mybir.ActivationFunctionType.Relu
-MULT = mybir.AluOpType.mult
+ADD, MAX, MULT = mybir.AluOpType.add, mybir.AluOpType.max, mybir.AluOpType.mult
 
 P = 128
 S = 512
@@ -13,6 +12,7 @@ Q = N // E
 HB = 2
 MB = 2
 COLS = Q // 16
+WARM_UPS = 4
 
 FLOPS = 2 * N * P * (HB * P) + 2 * N * (HB * P) * (MB * P)
 
@@ -24,53 +24,68 @@ def tile_rows_ffnback_relu_kernel(tc, base, x, w, b, w2, c, offs, out):
         tc.psum_pool(name="psum", bufs=1) as psum,
     ):
         base_t = held.tile([P, MB, S], BF16)
-        nc.sync.dma_start(base_t[:], base.rearrange("(a p) s -> p a s", p=P))
-        x_t = held.tile([P, N], BF16)
-        nc.scalar.dma_start(x_t[:], x)
-        w_t = held.tile([P, E, HB * P], BF16)
-        nc.scalar.dma_start(w_t[:], w.rearrange("e k h -> k e h"))
-        w2_t = held.tile([P, E * HB, MB * P], BF16)
-        nc.sync.dma_start(w2_t[:], w2.rearrange("e (a p) m -> p (e a) m", p=P))
+        nc.sync.dma_start(base_t[:], base.rearrange("(p a) s -> p a s", a=MB))
+        w2_t = held.tile([P, E, HB, P, MB], BF16)
+        nc.sync.dma_start(w2_t[:], w2.rearrange("e (p a) (m d) -> p e a m d", a=HB, d=MB))
         offsets = held.tile([P, N // 16], U16)
         nc.sync.dma_start(offsets[:], offs)
+        c_row = held.tile([1, N], F32)
+        nc.scalar.dma_start(c_row[:], c)
+        x_t = held.tile([P, N], BF16)
+        nc.scalar.dma_start(x_t[:], x)
+        w_t = held.tile([P, E, P, HB], BF16)
+        nc.scalar.dma_start(w_t[:], w.rearrange("e k (i a) -> k e i a", a=HB))
         b_t = held.tile([P, HB, E], F32)
-        nc.scalar.dma_start(b_t[:], b.rearrange("(a p) e -> p a e", p=P))
-        c_t = held.tile([P, N], F32)
-        nc.scalar.dma_start(c_t[:], c.rearrange("o t -> (o t)").partition_broadcast(P))
+        nc.scalar.dma_start(b_t[:], b.rearrange("(p a) e -> p a e", a=HB))
 
         ident = held.tile([P, P], BF16)
         make_identity(nc, ident[:])
 
-        windows = [psum.tile([P, S], F32, name=f"window{m}") for m in range(MB)]
-        for m in range(MB):
-            nc.tensor.matmul(windows[m][:], ident[:], base_t[:, m, :], start=True, stop=False)
+        zeros = held.tile([P, S], BF16)
+        nc.vector.memset(zeros[:], 0.0)
+        idle = psum.tile([P, S], F32)
+        for i in range(WARM_UPS):
+            nc.tensor.matmul(idle[:], zeros[:, 0:P], zeros[:], start=True, stop=True)
 
-        h = held.tile([P, E, HB, Q], BF16)
+        ones = held.tile([1, P], F32)
+        nc.vector.memset(ones[:], 1.0)
+        c_all = psum.tile([P, N], F32)
+        nc.tensor.matmul(c_all[:], ones[:], c_row[:], start=True, stop=True)
+        c_t = held.tile([P, N], F32)
+        nc.vector.tensor_copy(c_t[:], c_all[:])
+
+        pre = [psum.tile([P, HB, Q], F32, name=f"pre{e}") for e in range(E)]
         for e in range(E):
-            entries = slice(e * Q, (e + 1) * Q)
-            pre = psum.tile([P, HB, Q], F32, name=f"pre{e}")
+            for a in range(HB):
+                nc.tensor.matmul(pre[e][:, a, :], w_t[:, e, :, a], x_t[:, e * Q : (e + 1) * Q], start=True, stop=True)
+
+        windows = [psum.tile([P, S], F32, name=f"window{d}") for d in range(MB)]
+        for d in range(MB):
+            nc.tensor.matmul(windows[d][:], ident[:], base_t[:, d, :], start=True, stop=False)
+
+        h = [held.tile([P, HB, Q], BF16, name=f"h{e}") for e in range(E)]
+        for e in range(E):
             act = held.tile([P, HB, Q], F32, name=f"act{e}")
             for a in range(HB):
-                nc.tensor.matmul(pre[:, a, :], w_t[:, e, a * P : (a + 1) * P], x_t[:, entries], start=True, stop=True)
-            for a in range(HB):
-                nc.scalar.activation(act[:, a, :], pre[:, a, :], RELU, bias=b_t[:, a, e : e + 1])
-            for a in range(HB):
-                nc.vector.tensor_tensor(h[:, e, a, :], act[:, a, :], c_t[:, entries], MULT)
+                nc.vector.tensor_scalar(act[:, a, :], pre[e][:, a, :], b_t[:, a, e : e + 1], 0.0, ADD, MAX)
+            c_e = c_t[:, e * Q : (e + 1) * Q].unsqueeze(1).broadcast_to([P, HB, Q])
+            nc.vector.tensor_tensor(h[e][:], act[:], c_e, MULT)
 
-        for m in range(MB):
-            for e in range(E):
+        for e in range(E):
+            for d in range(MB):
                 for a in range(HB):
                     nc.tensor.matmul(
-                        windows[m][:].indirect(offsets[:, e * COLS : (e + 1) * COLS]),
-                        w2_t[:, e * HB + a, m * P : (m + 1) * P],
-                        h[:, e, a, :],
+                        windows[d][:].indirect(offsets[:, e * COLS : (e + 1) * COLS]),
+                        w2_t[:, e, a, :, d],
+                        h[e][:, a, :],
                         start=False,
                         stop=(e == E - 1 and a == HB - 1),
                     )
 
+        out_rows = out.rearrange("(p d) s -> p d s", d=MB)
         z0 = held.tile([P, S], F32)
         nc.vector.tensor_copy(z0[:], windows[0][:])
-        nc.sync.dma_start(out[0:P, :], z0[:])
+        nc.sync.dma_start(out_rows[:, 0, :], z0[:])
         z1 = held.tile([P, S], F32)
         nc.scalar.copy(z1[:], windows[1][:])
-        nc.scalar.dma_start(out[P : 2 * P, :], z1[:])
+        nc.scalar.dma_start(out_rows[:, 1, :], z1[:])

@@ -41,11 +41,12 @@ def tile_rows_ffnback_relu_kernel(tc, base, x, w, b, w2, c, offs, out):
         ident = held.tile([P, P], BF16)
         make_identity(nc, ident[:])
 
-        zeros = held.tile([P, S], BF16)
+        zeros = held.tile([P, P], BF16)
         nc.vector.memset(zeros[:], 0.0)
-        idle = psum.tile([P, S], F32)
+        zeros_wide = zeros[:].unsqueeze(1).broadcast_to([P, S // P, P])
+        idle = psum.tile([P, S // P, P], F32)
         for i in range(WARM_UPS):
-            nc.tensor.matmul(idle[:], zeros[:, 0:P], zeros[:], start=True, stop=True)
+            nc.tensor.matmul(idle[:], zeros[:], zeros_wide, start=True, stop=True)
 
         ones = held.tile([1, P], F32)
         nc.vector.memset(ones[:], 1.0)
@@ -63,29 +64,28 @@ def tile_rows_ffnback_relu_kernel(tc, base, x, w, b, w2, c, offs, out):
         for d in range(MB):
             nc.tensor.matmul(windows[d][:], ident[:], base_t[:, d, :], start=True, stop=False)
 
-        h = [held.tile([P, HB, Q], BF16, name=f"h{e}") for e in range(E)]
+        h = held.tile([P, E, HB, Q], BF16)
+        act = held.tile([P, E, HB, Q], F32)
         for e in range(E):
-            act = held.tile([P, HB, Q], F32, name=f"act{e}")
             for a in range(HB):
-                nc.vector.tensor_scalar(act[:, a, :], pre[e][:, a, :], b_t[:, a, e : e + 1], 0.0, ADD, MAX)
-            c_e = c_t[:, e * Q : (e + 1) * Q].unsqueeze(1).broadcast_to([P, HB, Q])
-            nc.vector.tensor_tensor(h[e][:], act[:], c_e, MULT)
+                nc.vector.tensor_scalar(act[:, e, a, :], pre[e][:, a, :], b_t[:, a, e : e + 1], 0.0, ADD, MAX)
+                nc.vector.tensor_tensor(h[:, e, a, :], act[:, e, a, :], c_t[:, e * Q : (e + 1) * Q], MULT)
 
         for e in range(E):
-            for d in range(MB):
-                for a in range(HB):
+            for a in range(HB):
+                for d in range(MB):
                     nc.tensor.matmul(
                         windows[d][:].indirect(offsets[:, e * COLS : (e + 1) * COLS]),
                         w2_t[:, e, a, :, d],
-                        h[e][:, a, :],
+                        h[:, e, a, :],
                         start=False,
                         stop=(e == E - 1 and a == HB - 1),
                     )
 
         out_rows = out.rearrange("(p d) s -> p d s", d=MB)
         z0 = held.tile([P, S], F32)
-        nc.vector.tensor_copy(z0[:], windows[0][:])
-        nc.sync.dma_start(out_rows[:, 0, :], z0[:])
+        nc.scalar.copy(z0[:], windows[0][:])
+        nc.scalar.dma_start(out_rows[:, 0, :], z0[:])
         z1 = held.tile([P, S], F32)
-        nc.scalar.copy(z1[:], windows[1][:])
-        nc.scalar.dma_start(out_rows[:, 1, :], z1[:])
+        nc.vector.tensor_copy(z1[:], windows[1][:])
+        nc.sync.dma_start(out_rows[:, 1, :], z1[:])

@@ -23,20 +23,20 @@ def tile_rows_ffnback_relu_kernel(tc, base, x, w, b, w2, c, offs, out):
         tc.tile_pool(name="held", bufs=1) as held,
         tc.psum_pool(name="psum", bufs=1) as psum,
     ):
+        c_row = held.tile([1, N], F32)
+        nc.sync.dma_start(c_row[:], c)
+        x_t = held.tile([P, N], BF16)
+        nc.sync.dma_start(x_t[:], x)
+        w_t = held.tile([P, E, P, HB], BF16)
+        nc.sync.dma_start(w_t[:], w.rearrange("e k (i a) -> k e i a", a=HB))
+        b_t = held.tile([P, HB, E], F32)
+        nc.sync.dma_start(b_t[:], b.rearrange("(p a) e -> p a e", a=HB))
         base_t = held.tile([P, MB, S], BF16)
-        nc.sync.dma_start(base_t[:], base.rearrange("(p a) s -> p a s", a=MB))
-        w2_t = held.tile([P, E, HB, P, MB], BF16)
-        nc.sync.dma_start(w2_t[:], w2.rearrange("e (p a) (m d) -> p e a m d", a=HB, d=MB))
+        nc.sync.dma_start(base_t[:], base.rearrange("(p d) s -> p d s", d=MB))
         offsets = held.tile([P, N // 16], U16)
         nc.sync.dma_start(offsets[:], offs)
-        c_row = held.tile([1, N], F32)
-        nc.scalar.dma_start(c_row[:], c)
-        x_t = held.tile([P, N], BF16)
-        nc.scalar.dma_start(x_t[:], x)
-        w_t = held.tile([P, E, P, HB], BF16)
-        nc.scalar.dma_start(w_t[:], w.rearrange("e k (i a) -> k e i a", a=HB))
-        b_t = held.tile([P, HB, E], F32)
-        nc.scalar.dma_start(b_t[:], b.rearrange("(p a) e -> p a e", a=HB))
+        w2_t = held.tile([P, E, HB, P, MB], BF16)
+        nc.sync.dma_start(w2_t[:], w2.rearrange("e (p a) (m d) -> p e a m d", a=HB, d=MB))
 
         ident = held.tile([P, P], BF16)
         make_identity(nc, ident[:])

import concourse.mybir as mybir
from concourse.masks import make_identity

BF16, F32, U16 = mybir.dt.bfloat16, mybir.dt.float32, mybir.dt.uint16
ADD, MAX, MULT = mybir.AluOpType.add, mybir.AluOpType.max, mybir.AluOpType.mult

P = 128
S = 512
N = 128
E = 2
Q = N // E
HB = 2
MB = 2
COLS = Q // 16
WARM_UPS = 4

FLOPS = 2 * N * P * (HB * P) + 2 * N * (HB * P) * (MB * P)


def tile_rows_ffnback_relu_kernel(tc, base, x, w, b, w2, c, offs, out):
    nc = tc.nc
    with (
        tc.tile_pool(name="held", bufs=1) as held,
        tc.psum_pool(name="psum", bufs=1) as psum,
    ):
        c_row = held.tile([1, N], F32)
        nc.sync.dma_start(c_row[:], c)
        x_t = held.tile([P, N], BF16)
        nc.sync.dma_start(x_t[:], x)
        w_t = held.tile([P, E, P, HB], BF16)
        nc.sync.dma_start(w_t[:], w.rearrange("e k (i a) -> k e i a", a=HB))
        b_t = held.tile([P, HB, E], F32)
        nc.sync.dma_start(b_t[:], b.rearrange("(p a) e -> p a e", a=HB))
        base_t = held.tile([P, MB, S], BF16)
        nc.sync.dma_start(base_t[:], base.rearrange("(p d) s -> p d s", d=MB))
        offsets = held.tile([P, N // 16], U16)
        nc.sync.dma_start(offsets[:], offs)
        w2_t = held.tile([P, E, HB, P, MB], BF16)
        nc.sync.dma_start(w2_t[:], w2.rearrange("e (p a) (m d) -> p e a m d", a=HB, d=MB))

        ident = held.tile([P, P], BF16)
        make_identity(nc, ident[:])

        zeros = held.tile([P, P], BF16)
        nc.vector.memset(zeros[:], 0.0)
        zeros_wide = zeros[:].unsqueeze(1).broadcast_to([P, S // P, P])
        idle = psum.tile([P, S // P, P], F32)
        for i in range(WARM_UPS):
            nc.tensor.matmul(idle[:], zeros[:], zeros_wide, start=True, stop=True)

        ones = held.tile([1, P], F32)
        nc.vector.memset(ones[:], 1.0)
        c_all = psum.tile([P, N], F32)
        nc.tensor.matmul(c_all[:], ones[:], c_row[:], start=True, stop=True)
        c_t = held.tile([P, N], F32)
        nc.vector.tensor_copy(c_t[:], c_all[:])

        pre = [psum.tile([P, HB, Q], F32, name=f"pre{e}") for e in range(E)]
        for e in range(E):
            for a in range(HB):
                nc.tensor.matmul(pre[e][:, a, :], w_t[:, e, :, a], x_t[:, e * Q : (e + 1) * Q], start=True, stop=True)

        windows = [psum.tile([P, S], F32, name=f"window{d}") for d in range(MB)]
        for d in range(MB):
            nc.tensor.matmul(windows[d][:], ident[:], base_t[:, d, :], start=True, stop=False)

        h = held.tile([P, E, HB, Q], BF16)
        act = held.tile([P, E, HB, Q], F32)
        for e in range(E):
            for a in range(HB):
                nc.vector.tensor_scalar(act[:, e, a, :], pre[e][:, a, :], b_t[:, a, e : e + 1], 0.0, ADD, MAX)
                nc.vector.tensor_tensor(h[:, e, a, :], act[:, e, a, :], c_t[:, e * Q : (e + 1) * Q], MULT)

        for e in range(E):
            for a in range(HB):
                for d in range(MB):
                    nc.tensor.matmul(
                        windows[d][:].indirect(offsets[:, e * COLS : (e + 1) * COLS]),
                        w2_t[:, e, a, :, d],
                        h[:, e, a, :],
                        start=False,
                        stop=(e == E - 1 and a == HB - 1),
                    )

        out_rows = out.rearrange("(p d) s -> p d s", d=MB)
        z0 = held.tile([P, S], F32)
        nc.scalar.copy(z0[:], windows[0][:])
        nc.scalar.dma_start(out_rows[:, 0, :], z0[:])
        z1 = held.tile([P, S], F32)
        nc.vector.tensor_copy(z1[:], windows[1][:])
        nc.sync.dma_start(out_rows[:, 1, :], z1[:])
